import numpy as np
import ml_dtypes


def mxq(x, axis, fmt="e4m3"):
    dtype, down = {"e4m3": (ml_dtypes.float8_e4m3fn, 7), "e5m2": (ml_dtypes.float8_e5m2, 14)}[fmt]
    v = np.moveaxis(np.asarray(x, np.float32).astype(ml_dtypes.bfloat16).astype(np.float64), axis, -1)
    blocks = v.reshape(v.shape[:-1] + (-1, 32))
    amax = np.abs(blocks).max(-1, keepdims=True)
    byte = np.maximum(np.where(amax > 0, np.frexp(amax)[1] - 1 + 127, 0) - down, 1)
    scale = np.exp2(byte - 127.0)
    codes = (blocks / scale).astype(np.float32).astype(dtype).astype(np.float64)
    return np.moveaxis((codes * scale).reshape(v.shape), -1, axis)


WIDE = False


def mx_kscale(k):
    if not WIDE:
        return np.ones(k)
    levels = np.array([10, -10, 5, -5, 0])
    if k % 512:
        return np.exp2(np.random.permutation(np.resize(levels, k // 32))).repeat(32)
    a = np.empty((k // 512, 16))
    for p in range(k // 512):
        a[p, :8] = np.random.permutation(np.resize(levels, 8))
        for g in range(8):
            far = levels[np.abs(levels - a[p, g]) >= 10]
            a[p, g + 8] = far[np.random.randint(len(far))]
    return np.exp2(a.ravel()).repeat(32)


def f64(x):
    return np.asarray(x).astype(np.float64)


def striped(idx):
    return np.tile(idx.reshape(-1, 16).T, (8, 1)).astype(np.uint16)


def unstriped(offs):
    return offs[:16].T.reshape(-1).astype(np.int64)


def pack_weight(w):
    k, n = w.shape
    w = f64(np.asarray(w, np.float32).astype(ml_dtypes.bfloat16)).reshape(k // 32, 32, n)
    amax = np.abs(w).max(1)
    byte = np.clip(np.where(amax > 0, np.frexp(amax)[1] - 1 + 127 - 7, 1), 1, 254)
    scaled = (w * np.exp2(127.0 - byte)[:, None, :]).reshape(k, n).astype(np.float32)
    words = np.ascontiguousarray(scaled.reshape(k // 512, 128, 4, n).transpose(0, 1, 3, 2)).astype(ml_dtypes.float8_e4m3fn).view(np.uint8)
    return words, np.ascontiguousarray(byte.astype(np.uint8).reshape(k // 512, 16, n))


def unpack_weight(words, scales):
    g, p, n, _ = words.shape
    vals = np.ascontiguousarray(words).view(ml_dtypes.float8_e4m3fn).astype(np.float64) * np.repeat(np.exp2(scales.astype(np.float64) - 127.0), 8, axis=1)[..., None]
    return vals.transpose(0, 1, 3, 2).reshape(g * 512, n)


K, T, S, D, N, H, V, U = 1024, 2048, 1024, 4, 128, 512, 256, 512


def setup_inputs():
    n = np.random.standard_normal
    s = mx_kscale(K)[:, None]
    u = mx_kscale(H)
    packed_xT = pack_weight(n((K, T)) * s)
    return {
        "x_words": packed_xT[0],
        "x_scales": packed_xT[1],
        "w1": (n((K, H)) / np.sqrt(K) / s).astype(np.float32),
        "w2": (n((K, H)) / np.sqrt(K) / s).astype(np.float32),
        "ref": (0.6 * n((H, S))).astype(np.float32),
        "unit": (np.random.uniform(0.6, 1.4, (H, 1)) * u[:, None]).astype(np.float32),
        "w3": (n((H, N)) / np.sqrt(H) / u[:, None]).astype(np.float32),
        "offs": striped(np.random.permutation(T)[:S]),
        "nl": striped(np.random.permutation(S)),
        "lib": striped(np.random.permutation(np.concatenate([np.arange(V), np.random.randint(0, V, U - V)]))),
    }


def reference(x_words, x_scales, w1, w2, ref, unit, w3, offs, nl, lib):
    xq = unpack_weight(x_words, x_scales)[:, unstriped(offs)]
    it = mxq(f64(w1), 0, "e4m3").T @ xq
    inten = np.log(np.exp(it) + 1.0)
    in_ = inten[:, unstriped(nl)]
    mz = mxq(f64(w2), 0, "e4m3").T @ xq
    mzz = np.tanh(mz)
    mn = mzz[:, unstriped(nl)]
    loss = mzz - mn
    mtch = np.exp(-1.5 * ((loss - f64(ref)) ** 2))
    psc = np.sqrt(inten * in_) * mtch
    tot = psc.reshape(len(psc), -1, D).sum(axis=2)
    tl = tot[:, unstriped(lib)]
    norm = inten.reshape(len(inten), -1, D).sum(axis=2)
    nl2 = norm[:, unstriped(lib)]
    hid = f64(unit) * (tl / (nl2 + 0.3))
    return mxq(f64(w3), 0, "e4m3").T @ mxq(hid, 0, "e4m3")

@@ -1,0 +1,275 @@
+import math
+from contextlib import ExitStack
+
+import concourse.mybir as mybir
+from concourse.masks import make_identity
+
+F32 = mybir.dt.float32
+BF16 = mybir.dt.bfloat16
+I32 = mybir.dt.int32
+U32 = mybir.dt.uint32
+U16 = mybir.dt.uint16
+U8 = mybir.dt.uint8
+FP8X4 = mybir.dt.float8_e4m3fn_x4
+ACT = mybir.ActivationFunctionType
+ALU = mybir.AluOpType
+
+K, T, S, D, N, H, V, U = 1024, 2048, 1024, 4, 128, 512, 256, 512
+P = 128
+PACK = 4
+K_PASS = P * PACK
+PASSES = K // K_PASS
+TILES = H // P
+BANK = 512
+HALVES = S // BANK
+LIST_ROWS = 16
+OUT_PARTS = 2
+OUT_COLS = U // OUT_PARTS
+LIB_WINDOW = 2 * OUT_COLS
+WORK_BUFS = 4
+SOFTPLUS_CAP = 40.0
+LOG_FLOOR = 2.0**-63
+
+FLOPS = 2 * 2 * K * H * S + 2 * H * N * U
+
+
+def tile_picked_ybioms_cos_p_kernel(tc, x_words, x_scales, w1, w2, ref, unit, w3, offs, nl, lib, out):
+    nc = tc.nc
+    with ExitStack() as ctx:
+        keep = ctx.enter_context(tc.tile_pool(name="keep", bufs=1))
+        ring = ctx.enter_context(tc.tile_pool(name="ring", bufs=2))
+        psum = ctx.enter_context(tc.psum_pool(name="psum", bufs=1))
+
+        def bank(index, name):
+            return psum.tile([P, BANK], F32, name=name, tag="bank%d" % index)
+
+        def entries(list_tile, first, count):
+            return list_tile[:, first // LIST_ROWS : (first + count) // LIST_ROWS]
+
+        def cols(h):
+            return slice(h * BANK, (h + 1) * BANK)
+
+        offs_sb = keep.tile([P, S // LIST_ROWS], U16, name="offs_sb")
+        nl_sb = keep.tile([P, S // LIST_ROWS], U16, name="nl_sb")
+        lib_sb = keep.tile([P, U // LIST_ROWS], U16, name="lib_sb")
+        x_table = [keep.tile([P, T], I32, name="x_table%d" % o) for o in range(PASSES)]
+        scale_table = keep.tile([P, T], U8, name="scale_table")
+        w1_raw = [keep.tile([P, PACK, H], F32, name="w1_raw%d" % o) for o in range(PASSES)]
+        w2_raw = [keep.tile([P, PACK, H], F32, name="w2_raw%d" % o) for o in range(PASSES)]
+        w3_raw = keep.tile([P, PACK, N], F32, name="w3_raw")
+        ref_sb = [keep.tile([P, S], F32, name="ref_sb%d" % t) for t in range(TILES)]
+        unit_sb = keep.tile([P, TILES], F32, name="unit_sb")
+        identity = keep.tile([P, P], F32, name="identity")
+        ratio = [keep.tile([P, LIB_WINDOW], F32, name="ratio%d" % t) for t in range(TILES)]
+
+        def load_x(o):
+            nc.sync.dma_start(out=x_table[o][:], in_=x_words[o].rearrange("p n t -> p (n t)").bitcast(I32))
+
+        def load_w(raw, w, o):
+            nc.sync.dma_start(out=raw[o][:], in_=w[o * K_PASS : (o + 1) * K_PASS, :].rearrange("(p j) c -> p j c", j=PACK))
+
+        def load_ref(t):
+            nc.sync.dma_start(out=ref_sb[t][:], in_=ref.rearrange("(p t) j -> p t j", t=TILES)[:, t, :])
+
+        nc.vector.memset(scale_table[:].bitcast(I32), 0)
+        load_w(w2_raw, w2, 0)
+        nc.sync.dma_start(offs_sb[:], offs)
+        for q in range(4):
+            nc.sync.dma_start(
+                out=scale_table[32 * q : 32 * q + 4 * PASSES, :].bitcast(I32),
+                in_=x_scales[:, 4 * q : 4 * q + 4, :].bitcast(I32),
+            )
+        load_x(0)
+        load_w(w2_raw, w2, 1)
+        load_x(1)
+        load_w(w1_raw, w1, 0)
+        load_w(w1_raw, w1, 1)
+        nc.sync.dma_start(nl_sb[:], nl)
+        load_ref(0)
+        for t in range(1, TILES):
+            load_ref(t)
+        nc.sync.dma_start(out=w3_raw[:], in_=w3.rearrange("(p j) c -> p j c", j=PACK))
+        nc.sync.dma_start(out=unit_sb[:], in_=unit.rearrange("(p t) o -> p (t o)", t=TILES))
+        nc.sync.dma_start(lib_sb[:], lib)
+
+        make_identity(nc, identity[:])
+        for t in range(TILES):
+            nc.gpsimd.memset(ratio[t][:, V:LIB_WINDOW], 0.0)
+
+        x_codes = [keep.tile([P, S], U32, name="x_codes%d" % o, align_bytes=64) for o in range(PASSES)]
+        x_planes = keep.tile([P, S], U8, name="x_planes", align_bytes=64)
+
+        def gather_x(o, h):
+            nc.vector.tensor_copy(x_codes[o][:, cols(h)], x_table[o][:].bitcast(U32).indirect(entries(offs_sb, h * BANK, BANK)))
+
+        def round_w(copy, raw, name):
+            grouped = ring.tile([P, TILES, P, PACK], BF16, name=name, tag="grouped", align_bytes=64)
+            copy(out=grouped[:].rearrange("p t m j -> p m j t"), in_=raw[:].rearrange("p j (m t) -> p m j t", t=TILES))
+            return grouped
+
+        def quantize_w(grouped, name):
+            codes = keep.tile([P, H], U32, name=name + "_codes", align_bytes=64)
+            scales = keep.tile([P, H], U8, name=name + "_scales", align_bytes=64)
+            nc.vector.quantize_mx(out=codes[:].bitcast(FP8X4), scales=scales[:], in_=grouped[:].rearrange("p t m j -> p (t m j)"))
+            return codes, scales
+
+        def product(w_mx, t, h, name):
+            acc = bank(HALVES * t + h, name)
+            for o in range(PASSES):
+                codes, scales = w_mx[o]
+                nc.tensor.matmul_mx(
+                    out=acc[:],
+                    lhsT=codes[:, t * P : (t + 1) * P].bitcast(FP8X4),
+                    lhsT_scale=scales[:, t * P : (t + 1) * P],
+                    rhs=x_codes[o][:, cols(h)].bitcast(FP8X4),
+                    rhs_scale=x_planes[4 * o : P, cols(h)],
+                    start=(o == 0),
+                    stop=(o == PASSES - 1),
+                )
+            return acc
+
+        def turn(dst, src, start, stop):
+            nc.tensor.matmul(dst, lhsT=src, rhs=identity[:], is_transpose=True, start=start, stop=stop)
+
+        nc.vector.tensor_copy(x_planes[:], scale_table[:].indirect(offs_sb[:]))
+        w2_grouped0 = round_w(nc.scalar.copy, w2_raw[0], "w2_grouped0")
+        w2_grouped1 = round_w(nc.scalar.copy, w2_raw[1], "w2_grouped1")
+        gather_x(0, 0)
+        w2_mx = [quantize_w(w2_grouped0, "w2_0")]
+        gather_x(0, 1)
+        gather_x(1, 0)
+        w2_mx.append(quantize_w(w2_grouped1, "w2_1"))
+        gather_x(1, 1)
+
+        mzz = [keep.tile([P, S], F32, name="mzz%d" % t) for t in range(TILES)]
+        for t, h in ((0, 0), (1, 0), (0, 1), (1, 1), (2, 0), (2, 1), (3, 0), (3, 1)):
+            mz = product(w2_mx, t, h, "mz%d_%d" % (t, h))
+            nc.scalar.activation(mzz[t][:, cols(h)], mz[:], ACT.Tanh)
+
+        miss = [keep.tile([P, S], F32, name="miss%d" % t) for t in range(TILES)]
+
+        def mismatch(t, shifted):
+            nc.vector.tensor_tensor(shifted[:], mzz[t][:], ref_sb[t][:], ALU.subtract)
+            for h in range(HALVES):
+                nc.vector.tensor_tensor(miss[t][:, cols(h)], mzz[t][:].indirect(entries(nl_sb, h * BANK, BANK)), shifted[:, cols(h)], ALU.subtract)
+
+        def by_member(natural):
+            return natural.rearrange("p (v d) -> p d v", d=D)
+
+        w1_grouped0 = round_w(nc.vector.tensor_copy, w1_raw[0], "w1_grouped0")
+        w1_mx = [quantize_w(w1_grouped0, "w1_0")]
+        w1_grouped1 = round_w(nc.vector.tensor_copy, w1_raw[1], "w1_grouped1")
+        w1_mx.append(quantize_w(w1_grouped1, "w1_1"))
+
+        soft = keep.tile([P, TILES, HALVES, D, P], F32, name="soft", tag="soft")
+        inten = keep.tile([P, TILES, HALVES, D, P], F32, name="inten")
+        it = {}
+        for t in range(TILES):
+            for h in range(HALVES):
+                it[t, h] = product(w1_mx, t, h, "it%d_%d" % (t, h))
+                nc.scalar.activation(soft[:, t, h], by_member(it[t, h][:]), ACT.Exp)
+        for t in range(TILES - 1):
+            mismatch(t, ring.tile([P, S], F32, name="shifted%d" % t, tag="shifted"))
+
+        w3_grouped = keep.tile([P, N, PACK], BF16, name="w3_grouped", align_bytes=64)
+        nc.gpsimd.tensor_copy(out=w3_grouped[:], in_=w3_raw[:].rearrange("p j c -> p c j"))
+        w3_codes = keep.tile([P, N], U32, name="w3_codes", align_bytes=64)
+        w3_scales = keep.tile([P, N], U8, name="w3_scales", align_bytes=64)
+        nc.vector.quantize_mx(out=w3_codes[:].bitcast(FP8X4), scales=w3_scales[:], in_=w3_grouped[:].rearrange("p c j -> p (c j)"))
+
+        for t in range(TILES):
+            nc.scalar.activation(soft[:, t], soft[:, t], ACT.Ln, bias=1.0)
+        for t in range(TILES):
+            for h in range(HALVES):
+                nc.vector.scalar_tensor_tensor(inten[:, t, h], soft[:, t, h], SOFTPLUS_CAP, by_member(it[t, h][:]), ALU.min, ALU.max)
+        mismatch(TILES - 1, keep.tile([P, S], F32, name="shifted_last", tag="soft"))
+
+        log_inten = [keep.tile([P, S], F32, name="log_inten%d" % t) for t in range(TILES)]
+        exponent = {}
+        log_norm_back = []
+
+        def member(src, h, d):
+            return src[:, h * BANK + d : (h + 1) * BANK : D]
+
+        def open_exponent(t):
+            for h in range(HALVES):
+                exponent[t, h] = bank(2 + (HALVES * t + h) % 6, "exponent%d_%d" % (t, h))
+                for d in range(D):
+                    turn(exponent[t, h][:, d * P : (d + 1) * P], member(log_inten[t], h, d), d == 0, False)
+
+        norm = None
+        for t in range(TILES):
+            nc.scalar.activation(miss[t][:], miss[t][:], ACT.Square, scale=math.sqrt(3.0))
+            nc.scalar.activation(
+                log_inten[t][:].rearrange("p (h v d) -> p h v d", h=HALVES, d=D),
+                inten[:, t].rearrange("p h d v -> p h v d"),
+                ACT.Ln,
+                bias=LOG_FLOOR,
+            )
+            if t % 2 == 0:
+                norm = bank(t // 2, "norm%d" % t)
+            for h in range(HALVES):
+                g = HALVES * (t % 2) + h
+                for d in range(D):
+                    turn(norm[:, g * P : (g + 1) * P], inten[:, t, h, d], d == 0, d == D - 1)
+            if t % 2 == 1:
+                log_norm = ring.tile([P, BANK], F32, name="log_norm%d" % t, tag="log_norm")
+                nc.scalar.activation(log_norm[:], norm[:], ACT.Ln, bias=0.3)
+                back = bank(t // 2, "log_norm_back%d" % t)
+                for g in range(BANK // P):
+                    turn(back[:, g * P : (g + 1) * P], log_norm[:, g * P : (g + 1) * P], True, True)
+                log_norm_back.append(back)
+            if t < TILES - 1:
+                open_exponent(t)
+
+        picked = keep.tile([P, TILES, U], BF16, name="picked")
+        hid = keep.tile([P, U, PACK], BF16, name="hid", align_bytes=64)
+        inverse = []
+        for t in range(TILES):
+            if t == TILES - 1:
+                open_exponent(t)
+            psc = []
+            for h in range(HALVES):
+                partner = ring.tile([P, BANK], F32, name="partner%d_%d" % (t, h), tag="work", bufs=WORK_BUFS)
+                nc.vector.tensor_tensor(partner[:], log_inten[t][:].indirect(entries(nl_sb, h * BANK, BANK)), miss[t][:, cols(h)], ALU.subtract)
+                for d in range(D):
+                    turn(exponent[t, h][:, d * P : (d + 1) * P], member(partner, 0, d), False, d == D - 1)
+                psc.append(ring.tile([P, BANK], F32, name="psc%d_%d" % (t, h), tag="psc", bufs=4))
+                nc.scalar.activation(psc[h][:], exponent[t, h][:], ACT.Exp, scale=0.5)
+            if t % 2 == 0:
+                inverse.append(keep.tile([P, BANK], F32, name="inverse%d" % t, tag="inverse%d" % t))
+                nc.scalar.activation(inverse[t // 2][:], log_norm_back[t // 2][:], ACT.Exp, scale=-1.0)
+            tot = bank(t // 2, "tot%d" % t)
+            for h in range(HALVES):
+                for d in range(D):
+                    turn(tot[:, h * P : (h + 1) * P], psc[h][:, d * P : (d + 1) * P], d == 0, d == D - 1)
+            nc.vector.scalar_tensor_tensor(
+                ratio[t][:, 0:V], tot[:, 0:V], unit_sb[:, t : t + 1], inverse[t // 2][:, (t % 2) * V : (t % 2 + 1) * V], ALU.mult, ALU.mult
+            )
+            for part in range(OUT_PARTS):
+                slots = slice(part * OUT_COLS, (part + 1) * OUT_COLS)
+                window = ratio[t][:].indirect(entries(lib_sb, part * OUT_COLS, OUT_COLS))
+                if t == TILES - 1 and part == 0:
+                    nc.vector.tensor_copy(picked[:, t, slots], window)
+                else:
+                    nc.scalar.activation(picked[:, t, slots], window, ACT.Copy)
+
+        for part in range(OUT_PARTS):
+            slots = slice(part * OUT_COLS, (part + 1) * OUT_COLS)
+            nc.vector.tensor_copy(out=hid[:, slots, :], in_=picked[:, :, slots].rearrange("p t r -> p r t"))
+            hid_codes = ring.tile([P, OUT_COLS], U32, name="hid_codes%d" % part, tag="hid_codes", align_bytes=64)
+            hid_scales = ring.tile([P, OUT_COLS], U8, name="hid_scales%d" % part, tag="hid_scales", align_bytes=64)
+            nc.vector.quantize_mx(out=hid_codes[:].bitcast(FP8X4), scales=hid_scales[:], in_=hid[:, slots, :].rearrange("p r t -> p (r t)"))
+            acc = bank(HALVES * part + 1, "out_acc%d" % part)
+            nc.tensor.matmul_mx(
+                out=acc[:, 0:OUT_COLS],
+                lhsT=w3_codes[:].bitcast(FP8X4),
+                lhsT_scale=w3_scales[:],
+                rhs=hid_codes[:].bitcast(FP8X4),
+                rhs_scale=hid_scales[:],
+                start=True,
+                stop=True,
+            )
+            result = ring.tile([P, OUT_COLS], F32, name="result%d" % part, tag="result")
+            nc.scalar.copy(out=result[:], in_=acc[:, 0:OUT_COLS])
+            nc.sync.dma_start(out=out[:, slots], in_=result[:])

@@ -27,6 +27,10 @@ OUT_PARTS = 2
 OUT_COLS = U // OUT_PARTS
 LIB_WINDOW = 2 * OUT_COLS
 WORK_BUFS = 4
+EARLY = 8
+HELD = {(3, 1): "inverse0"}
+SQUARE_LAG = 1
+ONV = [(3, 0)]
 SOFTPLUS_CAP = 40.0
 LOG_FLOOR = 2.0**-63
 
@@ -72,7 +76,6 @@ def tile_picked_ybioms_cos_p_kernel(tc, x_words, x_scales, w1, w2, ref, unit, w3
             nc.sync.dma_start(out=ref_sb[t][:], in_=ref.rearrange("(p t) j -> p t j", t=TILES)[:, t, :])
 
         nc.vector.memset(scale_table[:].bitcast(I32), 0)
-        load_w(w2_raw, w2, 0)
         nc.sync.dma_start(offs_sb[:], offs)
         for q in range(4):
             nc.sync.dma_start(
@@ -80,15 +83,17 @@ def tile_picked_ybioms_cos_p_kernel(tc, x_words, x_scales, w1, w2, ref, unit, w3
                 in_=x_scales[:, 4 * q : 4 * q + 4, :].bitcast(I32),
             )
         load_x(0)
-        load_w(w2_raw, w2, 1)
+        load_w(w2_raw, w2, 0)
         load_x(1)
+        load_w(w2_raw, w2, 1)
         load_w(w1_raw, w1, 0)
         load_w(w1_raw, w1, 1)
         nc.sync.dma_start(nl_sb[:], nl)
         load_ref(0)
-        for t in range(1, TILES):
-            load_ref(t)
         nc.sync.dma_start(out=w3_raw[:], in_=w3.rearrange("(p j) c -> p j c", j=PACK))
+        load_ref(1)
+        load_ref(2)
+        load_ref(3)
         nc.sync.dma_start(out=unit_sb[:], in_=unit.rearrange("(p t) o -> p (t o)", t=TILES))
         nc.sync.dma_start(lib_sb[:], lib)
 
@@ -102,15 +107,23 @@ def tile_picked_ybioms_cos_p_kernel(tc, x_words, x_scales, w1, w2, ref, unit, w3
         def gather_x(o, h):
             nc.vector.tensor_copy(x_codes[o][:, cols(h)], x_table[o][:].bitcast(U32).indirect(entries(offs_sb, h * BANK, BANK)))
 
-        def round_w(copy, raw, name):
+        def round_w(raw, on_vector, name):
             grouped = ring.tile([P, TILES, P, PACK], BF16, name=name, tag="grouped", align_bytes=64)
-            copy(out=grouped[:].rearrange("p t m j -> p m j t"), in_=raw[:].rearrange("p j (m t) -> p m j t", t=TILES))
+            dst = grouped[:].rearrange("p t m j -> p m j t")
+            src = raw[:].rearrange("p j (m t) -> p m j t", t=TILES)
+            if on_vector > 0:
+                nc.vector.tensor_copy(out=dst[:, 0:on_vector], in_=src[:, 0:on_vector])
+            if on_vector < P:
+                nc.scalar.copy(out=dst[:, on_vector:P], in_=src[:, on_vector:P])
             return grouped
 
-        def quantize_w(grouped, name):
+        def quantize_w(grouped, pieces, name):
             codes = keep.tile([P, H], U32, name=name + "_codes", align_bytes=64)
             scales = keep.tile([P, H], U8, name=name + "_scales", align_bytes=64)
-            nc.vector.quantize_mx(out=codes[:].bitcast(FP8X4), scales=scales[:], in_=grouped[:].rearrange("p t m j -> p (t m j)"))
+            values = grouped[:].rearrange("p t m j -> p (t m j)")
+            width = H // pieces
+            for c in range(0, H, width):
+                nc.vector.quantize_mx(out=codes[:, c : c + width].bitcast(FP8X4), scales=scales[:, c : c + width], in_=values[:, PACK * c : PACK * (c + width)])
             return codes, scales
 
         def product(w_mx, t, h, name):
@@ -132,57 +145,77 @@ def tile_picked_ybioms_cos_p_kernel(tc, x_words, x_scales, w1, w2, ref, unit, w3
             nc.tensor.matmul(dst, lhsT=src, rhs=identity[:], is_transpose=True, start=start, stop=stop)
 
         nc.vector.tensor_copy(x_planes[:], scale_table[:].indirect(offs_sb[:]))
-        w2_grouped0 = round_w(nc.scalar.copy, w2_raw[0], "w2_grouped0")
-        w2_grouped1 = round_w(nc.scalar.copy, w2_raw[1], "w2_grouped1")
         gather_x(0, 0)
-        w2_mx = [quantize_w(w2_grouped0, "w2_0")]
         gather_x(0, 1)
+        w2_mx = [quantize_w(round_w(w2_raw[0], 80, "w2_grouped0"), 1, "w2_0")]
         gather_x(1, 0)
-        w2_mx.append(quantize_w(w2_grouped1, "w2_1"))
         gather_x(1, 1)
+        w2_mx.append(quantize_w(round_w(w2_raw[1], 80, "w2_grouped1"), 1, "w2_1"))
 
         mzz = [keep.tile([P, S], F32, name="mzz%d" % t) for t in range(TILES)]
-        for t, h in ((0, 0), (1, 0), (0, 1), (1, 1), (2, 0), (2, 1), (3, 0), (3, 1)):
-            mz = product(w2_mx, t, h, "mz%d_%d" % (t, h))
-            nc.scalar.activation(mzz[t][:, cols(h)], mz[:], ACT.Tanh)
-
-        miss = [keep.tile([P, S], F32, name="miss%d" % t) for t in range(TILES)]
-
-        def mismatch(t, shifted):
-            nc.vector.tensor_tensor(shifted[:], mzz[t][:], ref_sb[t][:], ALU.subtract)
+        for t in range(TILES):
             for h in range(HALVES):
-                nc.vector.tensor_tensor(miss[t][:, cols(h)], mzz[t][:].indirect(entries(nl_sb, h * BANK, BANK)), shifted[:, cols(h)], ALU.subtract)
+                mz = product(w2_mx, t, h, "mz%d_%d" % (t, h))
+                nc.scalar.activation(mzz[t][:, cols(h)], mz[:], ACT.Tanh)
+
+        miss = {}
+        shifted = {}
+
+        def shift(t, tag):
+            shifted[t] = keep.tile([P, S], F32, name="shifted%d" % t, tag=tag)
+            nc.vector.tensor_tensor(shifted[t][:], mzz[t][:], ref_sb[t][:], ALU.subtract)
+
+        def mismatch(t, h, tag):
+            miss[t, h] = keep.tile([P, BANK], F32, name="miss%d_%d" % (t, h), tag=tag)
+            nc.vector.tensor_tensor(miss[t, h][:], mzz[t][:].indirect(entries(nl_sb, h * BANK, BANK)), shifted[t][:, cols(h)], ALU.subtract)
 
         def by_member(natural):
             return natural.rearrange("p (v d) -> p d v", d=D)
 
-        w1_grouped0 = round_w(nc.vector.tensor_copy, w1_raw[0], "w1_grouped0")
-        w1_mx = [quantize_w(w1_grouped0, "w1_0")]
-        w1_grouped1 = round_w(nc.vector.tensor_copy, w1_raw[1], "w1_grouped1")
-        w1_mx.append(quantize_w(w1_grouped1, "w1_1"))
+        w1_grouped0 = round_w(w1_raw[0], 128, "w1_grouped0")
+        w1_mx = [quantize_w(w1_grouped0, 1, "w1_0")]
+        w1_grouped1 = round_w(w1_raw[1], 128, "w1_grouped1")
+        w1_mx.append(quantize_w(w1_grouped1, 1, "w1_1"))
 
-        soft = keep.tile([P, TILES, HALVES, D, P], F32, name="soft", tag="soft")
+        soft = [keep.tile([P, HALVES, D, P], F32, name="soft%d" % t) for t in range(TILES)]
         inten = keep.tile([P, TILES, HALVES, D, P], F32, name="inten")
         it = {}
         for t in range(TILES):
             for h in range(HALVES):
                 it[t, h] = product(w1_mx, t, h, "it%d_%d" % (t, h))
-                nc.scalar.activation(soft[:, t, h], by_member(it[t, h][:]), ACT.Exp)
-        for t in range(TILES - 1):
-            mismatch(t, ring.tile([P, S], F32, name="shifted%d" % t, tag="shifted"))
+                nc.scalar.activation(soft[t][:, h], by_member(it[t, h][:]), ACT.Exp)
+        steps = []
+        for t in range(TILES):
+            steps.extend([(t, None), (t, 0), (t, 1)])
+
+        def step(t, h, tag):
+            if h is None:
+                shift(t, tag or "shifted%d" % (t % 2))
+            else:
+                mismatch(t, h, tag or "miss%d_%d" % (t, h))
+
+        for t, h in steps[:EARLY]:
+            step(t, h, None)
 
         w3_grouped = keep.tile([P, N, PACK], BF16, name="w3_grouped", align_bytes=64)
-        nc.gpsimd.tensor_copy(out=w3_grouped[:], in_=w3_raw[:].rearrange("p j c -> p c j"))
+        nc.scalar.copy(out=w3_grouped[:], in_=w3_raw[:].rearrange("p j c -> p c j"))
         w3_codes = keep.tile([P, N], U32, name="w3_codes", align_bytes=64)
         w3_scales = keep.tile([P, N], U8, name="w3_scales", align_bytes=64)
         nc.vector.quantize_mx(out=w3_codes[:].bitcast(FP8X4), scales=w3_scales[:], in_=w3_grouped[:].rearrange("p c j -> p (c j)"))
 
         for t in range(TILES):
-            nc.scalar.activation(soft[:, t], soft[:, t], ACT.Ln, bias=1.0)
+            nc.scalar.activation(soft[t][:], soft[t][:], ACT.Ln, bias=1.0)
         for t in range(TILES):
             for h in range(HALVES):
-                nc.vector.scalar_tensor_tensor(inten[:, t, h], soft[:, t, h], SOFTPLUS_CAP, by_member(it[t, h][:]), ALU.min, ALU.max)
-        mismatch(TILES - 1, keep.tile([P, S], F32, name="shifted_last", tag="soft"))
+                nc.vector.scalar_tensor_tensor(inten[:, t, h], soft[t][:, h], SOFTPLUS_CAP, by_member(it[t, h][:]), ALU.min, ALU.max)
+        norm = [bank(pair, "norm%d" % pair) for pair in range(TILES // 2)]
+        for t in range(TILES):
+            for h in range(HALVES):
+                g = HALVES * (t % 2) + h
+                for d in range(D):
+                    turn(norm[t // 2][:, g * P : (g + 1) * P], inten[:, t, h, d], d == 0, d == D - 1)
+        for n, (t, h) in enumerate(steps[EARLY:]):
+            step(t, h, "soft%d" % n if n < 2 else None)
 
         log_inten = [keep.tile([P, S], F32, name="log_inten%d" % t) for t in range(TILES)]
         exponent = {}
@@ -197,59 +230,78 @@ def tile_picked_ybioms_cos_p_kernel(tc, x_words, x_scales, w1, w2, ref, unit, w3
                 for d in range(D):
                     turn(exponent[t, h][:, d * P : (d + 1) * P], member(log_inten[t], h, d), d == 0, False)
 
-        norm = None
+        def square(t):
+            for h in range(HALVES):
+                nc.scalar.activation(miss[t, h][:], miss[t, h][:], ACT.Square, scale=math.sqrt(3.0))
+
         for t in range(TILES):
-            nc.scalar.activation(miss[t][:], miss[t][:], ACT.Square, scale=math.sqrt(3.0))
             nc.scalar.activation(
                 log_inten[t][:].rearrange("p (h v d) -> p h v d", h=HALVES, d=D),
                 inten[:, t].rearrange("p h d v -> p h v d"),
                 ACT.Ln,
                 bias=LOG_FLOOR,
             )
-            if t % 2 == 0:
-                norm = bank(t // 2, "norm%d" % t)
-            for h in range(HALVES):
-                g = HALVES * (t % 2) + h
-                for d in range(D):
-                    turn(norm[:, g * P : (g + 1) * P], inten[:, t, h, d], d == 0, d == D - 1)
+            if t >= SQUARE_LAG:
+                square(t - SQUARE_LAG)
             if t % 2 == 1:
                 log_norm = ring.tile([P, BANK], F32, name="log_norm%d" % t, tag="log_norm")
-                nc.scalar.activation(log_norm[:], norm[:], ACT.Ln, bias=0.3)
+                nc.scalar.activation(log_norm[:], norm[t // 2][:], ACT.Ln, bias=0.3)
                 back = bank(t // 2, "log_norm_back%d" % t)
                 for g in range(BANK // P):
                     turn(back[:, g * P : (g + 1) * P], log_norm[:, g * P : (g + 1) * P], True, True)
                 log_norm_back.append(back)
             if t < TILES - 1:
                 open_exponent(t)
+        for t in range(TILES - SQUARE_LAG, TILES):
+            square(t)
 
         picked = keep.tile([P, TILES, U], BF16, name="picked")
         hid = keep.tile([P, U, PACK], BF16, name="hid", align_bytes=64)
         inverse = []
-        for t in range(TILES):
-            if t == TILES - 1:
-                open_exponent(t)
-            psc = []
-            for h in range(HALVES):
+
+        def look_up_partner(t, h):
+            if (t, h) in HELD:
+                partner = keep.tile([P, BANK], F32, name="partner%d_%d" % (t, h), tag=HELD[t, h])
+            else:
                 partner = ring.tile([P, BANK], F32, name="partner%d_%d" % (t, h), tag="work", bufs=WORK_BUFS)
-                nc.vector.tensor_tensor(partner[:], log_inten[t][:].indirect(entries(nl_sb, h * BANK, BANK)), miss[t][:, cols(h)], ALU.subtract)
-                for d in range(D):
-                    turn(exponent[t, h][:, d * P : (d + 1) * P], member(partner, 0, d), False, d == D - 1)
-                psc.append(ring.tile([P, BANK], F32, name="psc%d_%d" % (t, h), tag="psc", bufs=4))
-                nc.scalar.activation(psc[h][:], exponent[t, h][:], ACT.Exp, scale=0.5)
-            if t % 2 == 0:
-                inverse.append(keep.tile([P, BANK], F32, name="inverse%d" % t, tag="inverse%d" % t))
-                nc.scalar.activation(inverse[t // 2][:], log_norm_back[t // 2][:], ACT.Exp, scale=-1.0)
-            tot = bank(t // 2, "tot%d" % t)
-            for h in range(HALVES):
-                for d in range(D):
-                    turn(tot[:, h * P : (h + 1) * P], psc[h][:, d * P : (d + 1) * P], d == 0, d == D - 1)
+            nc.vector.tensor_tensor(partner[:], log_inten[t][:].indirect(entries(nl_sb, h * BANK, BANK)), miss[t, h][:], ALU.subtract)
+            return partner
+
+        def score_tile(t, h):
+            return keep.tile([P, BANK], F32, name="psc%d_%d" % (t, h), tag="psc%d_%d" % (t % 2, h))
+
+        for t in range(TILES):
+            if t < TILES - 1:
+                psc = []
+                for h in range(HALVES):
+                    partner = look_up_partner(t, h)
+                    for d in range(D):
+                        turn(exponent[t, h][:, d * P : (d + 1) * P], member(partner, 0, d), False, d == D - 1)
+                    psc.append(score_tile(t, h))
+                    nc.scalar.activation(psc[h][:], exponent[t, h][:], ACT.Exp, scale=0.5)
+                if t % 2 == 0:
+                    for u in (t, t + 1):
+                        inverse.append(keep.tile([P, V], F32, name="inverse%d" % u, tag="inverse%d" % u))
+                        nc.scalar.activation(inverse[u][:], log_norm_back[t // 2][:, (u % 2) * V : (u % 2 + 1) * V], ACT.Exp, scale=-1.0)
+                tot = bank(t // 2, "tot%d" % t)
+                for h in range(HALVES):
+                    for d in range(D):
+                        turn(tot[:, h * P : (h + 1) * P], psc[h][:, d * P : (d + 1) * P], d == 0, d == D - 1)
+            else:
+                tot = keep.tile([P, V], F32, name="tot_last")
+                for h in range(HALVES):
+                    nc.vector.tensor_tensor(miss[t, h][:], miss[t, h][:], log_inten[t][:, cols(h)], ALU.subtract)
+                    partner = look_up_partner(t, h)
+                    score = score_tile(t, h)
+                    nc.scalar.activation(score[:], partner[:], ACT.Exp, scale=0.5)
+                    nc.vector.tensor_reduce(tot[:, h * P : (h + 1) * P], score[:].rearrange("p (v d) -> p v d", d=D), mybir.AxisListType.X, ALU.add)
             nc.vector.scalar_tensor_tensor(
-                ratio[t][:, 0:V], tot[:, 0:V], unit_sb[:, t : t + 1], inverse[t // 2][:, (t % 2) * V : (t % 2 + 1) * V], ALU.mult, ALU.mult
+                ratio[t][:, 0:V], tot[:, 0:V], unit_sb[:, t : t + 1], inverse[t][:], ALU.mult, ALU.mult
             )
             for part in range(OUT_PARTS):
                 slots = slice(part * OUT_COLS, (part + 1) * OUT_COLS)
                 window = ratio[t][:].indirect(entries(lib_sb, part * OUT_COLS, OUT_COLS))
-                if t == TILES - 1 and part == 0:
+                if (t, part) in ONV:
                     nc.vector.tensor_copy(picked[:, t, slots], window)
                 else:
                     nc.scalar.activation(picked[:, t, slots], window, ACT.Copy)

@@ -27,10 +27,13 @@ OUT_PARTS = 2
 OUT_COLS = U // OUT_PARTS
 LIB_WINDOW = 2 * OUT_COLS
 WORK_BUFS = 4
-EARLY = 8
-HELD = {(3, 1): "inverse0"}
+SHIFTS_ON_VECTOR = 1
+EARLY = 6
+TURNED = 3
+FUSED = []
+HELD = {}
 SQUARE_LAG = 1
-ONV = [(3, 0)]
+ONV = [(3, 0), (2, 0), (1, 0), (0, 0)]
 SOFTPLUS_CAP = 40.0
 LOG_FLOOR = 2.0**-63
 
@@ -88,12 +91,12 @@ def tile_picked_ybioms_cos_p_kernel(tc, x_words, x_scales, w1, w2, ref, unit, w3
         load_w(w2_raw, w2, 1)
         load_w(w1_raw, w1, 0)
         load_w(w1_raw, w1, 1)
-        nc.sync.dma_start(nl_sb[:], nl)
         load_ref(0)
-        nc.sync.dma_start(out=w3_raw[:], in_=w3.rearrange("(p j) c -> p j c", j=PACK))
+        nc.sync.dma_start(nl_sb[:], nl)
         load_ref(1)
         load_ref(2)
         load_ref(3)
+        nc.sync.dma_start(out=w3_raw[:], in_=w3.rearrange("(p j) c -> p j c", j=PACK))
         nc.sync.dma_start(out=unit_sb[:], in_=unit.rearrange("(p t) o -> p (t o)", t=TILES))
         nc.sync.dma_start(lib_sb[:], lib)
 
@@ -159,15 +162,17 @@ def tile_picked_ybioms_cos_p_kernel(tc, x_words, x_scales, w1, w2, ref, unit, w3
                 nc.scalar.activation(mzz[t][:, cols(h)], mz[:], ACT.Tanh)
 
         miss = {}
-        shifted = {}
 
-        def shift(t, tag):
-            shifted[t] = keep.tile([P, S], F32, name="shifted%d" % t, tag=tag)
-            nc.vector.tensor_tensor(shifted[t][:], mzz[t][:], ref_sb[t][:], ALU.subtract)
+        shifted = [keep.tile([P, S], F32, name="shifted%d" % t, tag="w2_raw%d" % t if t < PASSES else "shifted%d" % t) for t in range(TILES)]
+
+        def shift(t):
+            engine = nc.vector if t < SHIFTS_ON_VECTOR else nc.gpsimd
+            engine.tensor_tensor(shifted[t][:], mzz[t][:], ref_sb[t][:], ALU.subtract)
 
         def mismatch(t, h, tag):
-            miss[t, h] = keep.tile([P, BANK], F32, name="miss%d_%d" % (t, h), tag=tag)
-            nc.vector.tensor_tensor(miss[t, h][:], mzz[t][:].indirect(entries(nl_sb, h * BANK, BANK)), shifted[t][:, cols(h)], ALU.subtract)
+            miss[t, h] = keep.tile([P, BANK], F32, name="miss%d_%d" % (t, h), tag=tag, align_bytes=64)
+            nc.vector.tensor_copy(miss[t, h][:], mzz[t][:].indirect(entries(nl_sb, h * BANK, BANK)))
+            nc.gpsimd.tensor_tensor(miss[t, h][:], miss[t, h][:], shifted[t][:, cols(h)], ALU.subtract)
 
         def by_member(natural):
             return natural.rearrange("p (v d) -> p d v", d=D)
@@ -177,31 +182,18 @@ def tile_picked_ybioms_cos_p_kernel(tc, x_words, x_scales, w1, w2, ref, unit, w3
         w1_grouped1 = round_w(w1_raw[1], 128, "w1_grouped1")
         w1_mx.append(quantize_w(w1_grouped1, 1, "w1_1"))
 
-        soft = [keep.tile([P, HALVES, D, P], F32, name="soft%d" % t) for t in range(TILES)]
+        soft = [keep.tile([P, HALVES, D, P], F32, name="soft%d" % t, align_bytes=64) for t in range(TILES)]
         inten = keep.tile([P, TILES, HALVES, D, P], F32, name="inten")
         it = {}
         for t in range(TILES):
             for h in range(HALVES):
                 it[t, h] = product(w1_mx, t, h, "it%d_%d" % (t, h))
                 nc.scalar.activation(soft[t][:, h], by_member(it[t, h][:]), ACT.Exp)
-        steps = []
         for t in range(TILES):
-            steps.extend([(t, None), (t, 0), (t, 1)])
-
-        def step(t, h, tag):
-            if h is None:
-                shift(t, tag or "shifted%d" % (t % 2))
-            else:
-                mismatch(t, h, tag or "miss%d_%d" % (t, h))
-
+            shift(t)
+        steps = [(t, h) for t in range(TILES) for h in range(HALVES)]
         for t, h in steps[:EARLY]:
-            step(t, h, None)
-
-        w3_grouped = keep.tile([P, N, PACK], BF16, name="w3_grouped", align_bytes=64)
-        nc.scalar.copy(out=w3_grouped[:], in_=w3_raw[:].rearrange("p j c -> p c j"))
-        w3_codes = keep.tile([P, N], U32, name="w3_codes", align_bytes=64)
-        w3_scales = keep.tile([P, N], U8, name="w3_scales", align_bytes=64)
-        nc.vector.quantize_mx(out=w3_codes[:].bitcast(FP8X4), scales=w3_scales[:], in_=w3_grouped[:].rearrange("p c j -> p (c j)"))
+            mismatch(t, h, "miss%d_%d" % (t, h))
 
         for t in range(TILES):
             nc.scalar.activation(soft[t][:], soft[t][:], ACT.Ln, bias=1.0)
@@ -214,8 +206,15 @@ def tile_picked_ybioms_cos_p_kernel(tc, x_words, x_scales, w1, w2, ref, unit, w3
                 g = HALVES * (t % 2) + h
                 for d in range(D):
                     turn(norm[t // 2][:, g * P : (g + 1) * P], inten[:, t, h, d], d == 0, d == D - 1)
+
         for n, (t, h) in enumerate(steps[EARLY:]):
-            step(t, h, "soft%d" % n if n < 2 else None)
+            mismatch(t, h, "soft%d" % n)
+
+        w3_grouped = keep.tile([P, N, PACK], BF16, name="w3_grouped", tag="soft3", align_bytes=64)
+        nc.vector.tensor_copy(out=w3_grouped[:], in_=w3_raw[:].rearrange("p j c -> p c j"))
+        w3_codes = keep.tile([P, N], U32, name="w3_codes", align_bytes=64)
+        w3_scales = keep.tile([P, N], U8, name="w3_scales", align_bytes=64)
+        nc.vector.quantize_mx(out=w3_codes[:].bitcast(FP8X4), scales=w3_scales[:], in_=w3_grouped[:].rearrange("p c j -> p (c j)"))
 
         log_inten = [keep.tile([P, S], F32, name="log_inten%d" % t) for t in range(TILES)]
         exponent = {}
@@ -264,14 +263,20 @@ def tile_picked_ybioms_cos_p_kernel(tc, x_words, x_scales, w1, w2, ref, unit, w3
                 partner = keep.tile([P, BANK], F32, name="partner%d_%d" % (t, h), tag=HELD[t, h])
             else:
                 partner = ring.tile([P, BANK], F32, name="partner%d_%d" % (t, h), tag="work", bufs=WORK_BUFS)
-            nc.vector.tensor_tensor(partner[:], log_inten[t][:].indirect(entries(nl_sb, h * BANK, BANK)), miss[t, h][:], ALU.subtract)
+            if (t, h) in FUSED:
+                nc.vector.tensor_tensor(partner[:], log_inten[t][:].indirect(entries(nl_sb, h * BANK, BANK)), miss[t, h][:], ALU.subtract)
+            else:
+                nc.vector.tensor_copy(partner[:], log_inten[t][:].indirect(entries(nl_sb, h * BANK, BANK)))
+                nc.gpsimd.tensor_tensor(partner[:], partner[:], miss[t, h][:], ALU.subtract)
             return partner
 
         def score_tile(t, h):
             return keep.tile([P, BANK], F32, name="psc%d_%d" % (t, h), tag="psc%d_%d" % (t % 2, h))
 
         for t in range(TILES):
-            if t < TILES - 1:
+            if t < TURNED:
+                if t == TILES - 1:
+                    open_exponent(t)
                 psc = []
                 for h in range(HALVES):
                     partner = look_up_partner(t, h)
@@ -290,7 +295,7 @@ def tile_picked_ybioms_cos_p_kernel(tc, x_words, x_scales, w1, w2, ref, unit, w3
             else:
                 tot = keep.tile([P, V], F32, name="tot_last")
                 for h in range(HALVES):
-                    nc.vector.tensor_tensor(miss[t, h][:], miss[t, h][:], log_inten[t][:, cols(h)], ALU.subtract)
+                    nc.gpsimd.tensor_tensor(miss[t, h][:], miss[t, h][:], log_inten[t][:, cols(h)], ALU.subtract)
                     partner = look_up_partner(t, h)
                     score = score_tile(t, h)
                     nc.scalar.activation(score[:], partner[:], ACT.Exp, scale=0.5)

@@ -19,6 +19,8 @@ P = 128
 PACK = 4
 K_PASS = P * PACK
 PASSES = K // K_PASS
+QUADRANTS = 4
+SCALE_ROWS = 4
 TILES = H // P
 BANK = 512
 HALVES = S // BANK
@@ -26,14 +28,12 @@ LIST_ROWS = 16
 OUT_PARTS = 2
 OUT_COLS = U // OUT_PARTS
 LIB_WINDOW = 2 * OUT_COLS
-WORK_BUFS = 4
+W2_ROWS_ON_VECTOR = 80
+LAST_QUANTISE_PIECES = 2
+BANKS = 8
+PAIRS = 2
 SHIFTS_ON_VECTOR = 1
-EARLY = 6
-TURNED = 3
-FUSED = []
-HELD = {}
-SQUARE_LAG = 1
-ONV = [(3, 0), (2, 0), (1, 0), (0, 0)]
+EXPONENT_BANKS = 6
 SOFTPLUS_CAP = 40.0
 LOG_FLOOR = 2.0**-63
 
@@ -79,22 +79,22 @@ def tile_picked_ybioms_cos_p_kernel(tc, x_words, x_scales, w1, w2, ref, unit, w3
             nc.sync.dma_start(out=ref_sb[t][:], in_=ref.rearrange("(p t) j -> p t j", t=TILES)[:, t, :])
 
         nc.vector.memset(scale_table[:].bitcast(I32), 0)
-        nc.sync.dma_start(offs_sb[:], offs)
-        for q in range(4):
-            nc.sync.dma_start(
-                out=scale_table[32 * q : 32 * q + 4 * PASSES, :].bitcast(I32),
-                in_=x_scales[:, 4 * q : 4 * q + 4, :].bitcast(I32),
-            )
         load_x(0)
+        nc.sync.dma_start(offs_sb[:], offs)
+        for q in range(QUADRANTS):
+            nc.sync.dma_start(
+                out=scale_table[32 * q : 32 * q + SCALE_ROWS * PASSES, :].bitcast(I32),
+                in_=x_scales[:, SCALE_ROWS * q : SCALE_ROWS * (q + 1), :].bitcast(I32),
+            )
         load_w(w2_raw, w2, 0)
         load_x(1)
         load_w(w2_raw, w2, 1)
         load_w(w1_raw, w1, 0)
         load_w(w1_raw, w1, 1)
         load_ref(0)
-        nc.sync.dma_start(nl_sb[:], nl)
         load_ref(1)
         load_ref(2)
+        nc.sync.dma_start(nl_sb[:], nl)
         load_ref(3)
         nc.sync.dma_start(out=w3_raw[:], in_=w3.rearrange("(p j) c -> p j c", j=PACK))
         nc.sync.dma_start(out=unit_sb[:], in_=unit.rearrange("(p t) o -> p (t o)", t=TILES))
@@ -107,11 +107,12 @@ def tile_picked_ybioms_cos_p_kernel(tc, x_words, x_scales, w1, w2, ref, unit, w3
         x_codes = [keep.tile([P, S], U32, name="x_codes%d" % o, align_bytes=64) for o in range(PASSES)]
         x_planes = keep.tile([P, S], U8, name="x_planes", align_bytes=64)
 
-        def gather_x(o, h):
-            nc.vector.tensor_copy(x_codes[o][:, cols(h)], x_table[o][:].bitcast(U32).indirect(entries(offs_sb, h * BANK, BANK)))
+        def gather_x(o):
+            for h in range(HALVES):
+                nc.vector.tensor_copy(x_codes[o][:, cols(h)], x_table[o][:].bitcast(U32).indirect(entries(offs_sb, h * BANK, BANK)))
 
         def round_w(raw, on_vector, name):
-            grouped = ring.tile([P, TILES, P, PACK], BF16, name=name, tag="grouped", align_bytes=64)
+            grouped = keep.tile([P, TILES, P, PACK], BF16, name=name, align_bytes=64)
             dst = grouped[:].rearrange("p t m j -> p m j t")
             src = raw[:].rearrange("p j (m t) -> p m j t", t=TILES)
             if on_vector > 0:
@@ -138,22 +139,18 @@ def tile_picked_ybioms_cos_p_kernel(tc, x_words, x_scales, w1, w2, ref, unit, w3
                     lhsT=codes[:, t * P : (t + 1) * P].bitcast(FP8X4),
                     lhsT_scale=scales[:, t * P : (t + 1) * P],
                     rhs=x_codes[o][:, cols(h)].bitcast(FP8X4),
-                    rhs_scale=x_planes[4 * o : P, cols(h)],
+                    rhs_scale=x_planes[SCALE_ROWS * o : P, cols(h)],
                     start=(o == 0),
                     stop=(o == PASSES - 1),
                 )
             return acc
 
-        def turn(dst, src, start, stop):
-            nc.tensor.matmul(dst, lhsT=src, rhs=identity[:], is_transpose=True, start=start, stop=stop)
-
-        nc.vector.tensor_copy(x_planes[:], scale_table[:].indirect(offs_sb[:]))
-        gather_x(0, 0)
-        gather_x(0, 1)
-        w2_mx = [quantize_w(round_w(w2_raw[0], 80, "w2_grouped0"), 1, "w2_0")]
-        gather_x(1, 0)
-        gather_x(1, 1)
-        w2_mx.append(quantize_w(round_w(w2_raw[1], 80, "w2_grouped1"), 1, "w2_1"))
+        w2_mx = []
+        for o in range(PASSES):
+            gather_x(o)
+            if o == 0:
+                nc.vector.tensor_copy(x_planes[:], scale_table[:].indirect(offs_sb[:]))
+            w2_mx.append(quantize_w(round_w(w2_raw[o], (0, 32)[o], "w2_grouped%d" % o), 1, "w2_%d" % o))
 
         mzz = [keep.tile([P, S], F32, name="mzz%d" % t) for t in range(TILES)]
         for t in range(TILES):
@@ -161,163 +158,121 @@ def tile_picked_ybioms_cos_p_kernel(tc, x_words, x_scales, w1, w2, ref, unit, w3
                 mz = product(w2_mx, t, h, "mz%d_%d" % (t, h))
                 nc.scalar.activation(mzz[t][:, cols(h)], mz[:], ACT.Tanh)
 
-        miss = {}
+        w1_mx = [quantize_w(round_w(w1_raw[0], 64, "w1_grouped0"), 1, "w1_0")]
+        w1_mx.append(quantize_w(round_w(w1_raw[1], P, "w1_grouped1"), LAST_QUANTISE_PIECES, "w1_1"))
+        shifted_first = keep.tile([P, SHIFTS_ON_VECTOR, S], F32, name="shifted_first", tag="w1_grouped1", align_bytes=64)
+        shifted = [shifted_first[:, t] for t in range(SHIFTS_ON_VECTOR)]
+        for t in range(SHIFTS_ON_VECTOR):
+            nc.vector.tensor_tensor(shifted[t], mzz[t][:], ref_sb[t][:], ALU.subtract)
+        shifted_later = keep.tile([P, TILES - SHIFTS_ON_VECTOR, S], F32, name="shifted_later", tag="ref_sb%d" % (SHIFTS_ON_VECTOR - 1))
+        shifted.extend([shifted_later[:, t] for t in range(TILES - SHIFTS_ON_VECTOR)])
 
-        shifted = [keep.tile([P, S], F32, name="shifted%d" % t, tag="w2_raw%d" % t if t < PASSES else "shifted%d" % t) for t in range(TILES)]
-
-        def shift(t):
-            engine = nc.vector if t < SHIFTS_ON_VECTOR else nc.gpsimd
-            engine.tensor_tensor(shifted[t][:], mzz[t][:], ref_sb[t][:], ALU.subtract)
-
-        def mismatch(t, h, tag):
-            miss[t, h] = keep.tile([P, BANK], F32, name="miss%d_%d" % (t, h), tag=tag, align_bytes=64)
-            nc.vector.tensor_copy(miss[t, h][:], mzz[t][:].indirect(entries(nl_sb, h * BANK, BANK)))
-            nc.gpsimd.tensor_tensor(miss[t, h][:], miss[t, h][:], shifted[t][:, cols(h)], ALU.subtract)
-
-        def by_member(natural):
-            return natural.rearrange("p (v d) -> p d v", d=D)
-
-        w1_grouped0 = round_w(w1_raw[0], 128, "w1_grouped0")
-        w1_mx = [quantize_w(w1_grouped0, 1, "w1_0")]
-        w1_grouped1 = round_w(w1_raw[1], 128, "w1_grouped1")
-        w1_mx.append(quantize_w(w1_grouped1, 1, "w1_1"))
-
-        soft = [keep.tile([P, HALVES, D, P], F32, name="soft%d" % t, align_bytes=64) for t in range(TILES)]
-        inten = keep.tile([P, TILES, HALVES, D, P], F32, name="inten")
+        soft = [keep.tile([P, S], F32, name="soft%d" % t, align_bytes=64) for t in range(TILES)]
+        inten = [keep.tile([P, S], F32, name="inten%d" % t) for t in range(TILES)]
         it = {}
         for t in range(TILES):
             for h in range(HALVES):
                 it[t, h] = product(w1_mx, t, h, "it%d_%d" % (t, h))
-                nc.scalar.activation(soft[t][:, h], by_member(it[t, h][:]), ACT.Exp)
+                nc.scalar.activation(soft[t][:, cols(h)], it[t, h][:], ACT.Exp)
+
+        for t in range(SHIFTS_ON_VECTOR, TILES):
+            nc.gpsimd.tensor_tensor(shifted[t], mzz[t][:], ref_sb[t][:], ALU.subtract)
+        miss = {}
         for t in range(TILES):
-            shift(t)
-        steps = [(t, h) for t in range(TILES) for h in range(HALVES)]
-        for t, h in steps[:EARLY]:
-            mismatch(t, h, "miss%d_%d" % (t, h))
+            for h in range(HALVES):
+                miss[t, h] = keep.tile([P, BANK], F32, name="miss%d_%d" % (t, h), align_bytes=64)
+                nc.vector.tensor_copy(miss[t, h][:], mzz[t][:].indirect(entries(nl_sb, h * BANK, BANK)))
+                nc.gpsimd.tensor_tensor(miss[t, h][:], miss[t, h][:], shifted[t][:, cols(h)], ALU.subtract)
 
         for t in range(TILES):
             nc.scalar.activation(soft[t][:], soft[t][:], ACT.Ln, bias=1.0)
         for t in range(TILES):
             for h in range(HALVES):
-                nc.vector.scalar_tensor_tensor(inten[:, t, h], soft[t][:, h], SOFTPLUS_CAP, by_member(it[t, h][:]), ALU.min, ALU.max)
-        norm = [bank(pair, "norm%d" % pair) for pair in range(TILES // 2)]
-        for t in range(TILES):
-            for h in range(HALVES):
-                g = HALVES * (t % 2) + h
-                for d in range(D):
-                    turn(norm[t // 2][:, g * P : (g + 1) * P], inten[:, t, h, d], d == 0, d == D - 1)
-
-        for n, (t, h) in enumerate(steps[EARLY:]):
-            mismatch(t, h, "soft%d" % n)
-
-        w3_grouped = keep.tile([P, N, PACK], BF16, name="w3_grouped", tag="soft3", align_bytes=64)
-        nc.vector.tensor_copy(out=w3_grouped[:], in_=w3_raw[:].rearrange("p j c -> p c j"))
-        w3_codes = keep.tile([P, N], U32, name="w3_codes", align_bytes=64)
-        w3_scales = keep.tile([P, N], U8, name="w3_scales", align_bytes=64)
-        nc.vector.quantize_mx(out=w3_codes[:].bitcast(FP8X4), scales=w3_scales[:], in_=w3_grouped[:].rearrange("p c j -> p (c j)"))
+                nc.vector.scalar_tensor_tensor(inten[t][:, cols(h)], soft[t][:, cols(h)], SOFTPLUS_CAP, it[t, h][:], ALU.min, ALU.max)
 
         log_inten = [keep.tile([P, S], F32, name="log_inten%d" % t) for t in range(TILES)]
         exponent = {}
-        log_norm_back = []
 
-        def member(src, h, d):
-            return src[:, h * BANK + d : (h + 1) * BANK : D]
+        def turn(dst, src, start, stop):
+            nc.tensor.matmul(dst, lhsT=src, rhs=identity[:], is_transpose=True, start=start, stop=stop)
 
-        def open_exponent(t):
+        def add_turned(acc, src, opens):
+            for d in range(D):
+                turn(acc[:, d * P : (d + 1) * P], src[:, d:BANK:D], opens and d == 0, not opens and d == D - 1)
+
+        def open_exponent(t, h):
+            exponent[t, h] = bank(PAIRS + (HALVES * t + h) % EXPONENT_BANKS, "exponent%d_%d" % (t, h))
+            add_turned(exponent[t, h], log_inten[t][:, cols(h)], True)
+
+        norm_turned = bank(0, "norm_turned")
+        for t in range(PAIRS):
             for h in range(HALVES):
-                exponent[t, h] = bank(2 + (HALVES * t + h) % 6, "exponent%d_%d" % (t, h))
+                g = HALVES * t + h
                 for d in range(D):
-                    turn(exponent[t, h][:, d * P : (d + 1) * P], member(log_inten[t], h, d), d == 0, False)
+                    turn(norm_turned[:, g * P : (g + 1) * P], inten[t][:, h * BANK + d : (h + 1) * BANK : D], d == 0, d == D - 1)
+        inverse = keep.tile([P, TILES, V], F32, name="inverse", align_bytes=64)
+        for t in range(PAIRS, TILES):
+            nc.vector.tensor_reduce(inverse[:, t], inten[t][:].rearrange("p (v d) -> p v d", d=D), mybir.AxisListType.X, ALU.add)
 
         def square(t):
             for h in range(HALVES):
                 nc.scalar.activation(miss[t, h][:], miss[t, h][:], ACT.Square, scale=math.sqrt(3.0))
 
         for t in range(TILES):
-            nc.scalar.activation(
-                log_inten[t][:].rearrange("p (h v d) -> p h v d", h=HALVES, d=D),
-                inten[:, t].rearrange("p h d v -> p h v d"),
-                ACT.Ln,
-                bias=LOG_FLOOR,
-            )
-            if t >= SQUARE_LAG:
-                square(t - SQUARE_LAG)
-            if t % 2 == 1:
-                log_norm = ring.tile([P, BANK], F32, name="log_norm%d" % t, tag="log_norm")
-                nc.scalar.activation(log_norm[:], norm[t // 2][:], ACT.Ln, bias=0.3)
-                back = bank(t // 2, "log_norm_back%d" % t)
+            nc.scalar.activation(log_inten[t][:], inten[t][:], ACT.Ln, bias=LOG_FLOOR)
+            if t > 0:
+                square(t - 1)
+            if t == PAIRS - 1:
+                turned = keep.tile([P, BANK], F32, name="log_norm_turned")
+                nc.scalar.activation(turned[:], norm_turned[:], ACT.Ln, bias=0.3)
+                log_norm = bank(0, "log_norm")
                 for g in range(BANK // P):
-                    turn(back[:, g * P : (g + 1) * P], log_norm[:, g * P : (g + 1) * P], True, True)
-                log_norm_back.append(back)
-            if t < TILES - 1:
-                open_exponent(t)
-        for t in range(TILES - SQUARE_LAG, TILES):
-            square(t)
+                    turn(log_norm[:, g * P : (g + 1) * P], turned[:, g * P : (g + 1) * P], True, True)
+            for h in range(HALVES):
+                if HALVES * t + h < EXPONENT_BANKS:
+                    open_exponent(t, h)
+        nc.scalar.activation(inverse[:, PAIRS:TILES], inverse[:, PAIRS:TILES], ACT.Ln, bias=0.3)
+        square(TILES - 1)
+        nc.scalar.activation(inverse[:, 0:PAIRS].rearrange("p t v -> p (t v)"), log_norm[:], ACT.Exp, scale=-1.0)
+        nc.scalar.activation(inverse[:, PAIRS:TILES], inverse[:, PAIRS:TILES], ACT.Exp, scale=-1.0)
 
         picked = keep.tile([P, TILES, U], BF16, name="picked")
-        hid = keep.tile([P, U, PACK], BF16, name="hid", align_bytes=64)
-        inverse = []
-
-        def look_up_partner(t, h):
-            if (t, h) in HELD:
-                partner = keep.tile([P, BANK], F32, name="partner%d_%d" % (t, h), tag=HELD[t, h])
-            else:
-                partner = ring.tile([P, BANK], F32, name="partner%d_%d" % (t, h), tag="work", bufs=WORK_BUFS)
-            if (t, h) in FUSED:
-                nc.vector.tensor_tensor(partner[:], log_inten[t][:].indirect(entries(nl_sb, h * BANK, BANK)), miss[t, h][:], ALU.subtract)
-            else:
-                nc.vector.tensor_copy(partner[:], log_inten[t][:].indirect(entries(nl_sb, h * BANK, BANK)))
-                nc.gpsimd.tensor_tensor(partner[:], partner[:], miss[t, h][:], ALU.subtract)
-            return partner
-
-        def score_tile(t, h):
-            return keep.tile([P, BANK], F32, name="psc%d_%d" % (t, h), tag="psc%d_%d" % (t % 2, h))
-
         for t in range(TILES):
-            if t < TURNED:
-                if t == TILES - 1:
-                    open_exponent(t)
-                psc = []
-                for h in range(HALVES):
-                    partner = look_up_partner(t, h)
-                    for d in range(D):
-                        turn(exponent[t, h][:, d * P : (d + 1) * P], member(partner, 0, d), False, d == D - 1)
-                    psc.append(score_tile(t, h))
-                    nc.scalar.activation(psc[h][:], exponent[t, h][:], ACT.Exp, scale=0.5)
-                if t % 2 == 0:
-                    for u in (t, t + 1):
-                        inverse.append(keep.tile([P, V], F32, name="inverse%d" % u, tag="inverse%d" % u))
-                        nc.scalar.activation(inverse[u][:], log_norm_back[t // 2][:, (u % 2) * V : (u % 2 + 1) * V], ACT.Exp, scale=-1.0)
-                tot = bank(t // 2, "tot%d" % t)
-                for h in range(HALVES):
-                    for d in range(D):
-                        turn(tot[:, h * P : (h + 1) * P], psc[h][:, d * P : (d + 1) * P], d == 0, d == D - 1)
+            psc = []
+            for h in range(HALVES):
+                if HALVES * t + h >= EXPONENT_BANKS:
+                    open_exponent(t, h)
+                partner = ring.tile([P, BANK], F32, name="partner%d_%d" % (t, h), tag="partner", bufs=4)
+                nc.vector.tensor_tensor(partner[:], log_inten[t][:].indirect(entries(nl_sb, h * BANK, BANK)), miss[t, h][:], ALU.subtract)
+                add_turned(exponent[t, h], partner[:], False)
+                psc.append(keep.tile([P, BANK], F32, name="psc%d_%d" % (t, h), tag="psc%d_%d" % (t % 2, h)))
+                nc.scalar.activation(psc[h][:], exponent[t, h][:], ACT.Exp, scale=0.5)
+            tot = bank((t + 1) % PAIRS, "tot%d" % t)
+            for h in range(HALVES):
+                for d in range(D):
+                    turn(tot[:, h * P : (h + 1) * P], psc[h][:, d * P : (d + 1) * P], d == 0, d == D - 1)
+            nc.vector.scalar_tensor_tensor(ratio[t][:, 0:V], tot[:, 0:V], unit_sb[:, t : t + 1], inverse[:, t], ALU.mult, ALU.mult)
+            nc.vector.tensor_copy(picked[:, t, 0:OUT_COLS], ratio[t][:].indirect(entries(lib_sb, 0, OUT_COLS)))
+            second = ratio[t][:].indirect(entries(lib_sb, OUT_COLS, OUT_COLS))
+            if t < 0:
+                nc.vector.tensor_copy(picked[:, t, OUT_COLS:U], second)
             else:
-                tot = keep.tile([P, V], F32, name="tot_last")
-                for h in range(HALVES):
-                    nc.gpsimd.tensor_tensor(miss[t, h][:], miss[t, h][:], log_inten[t][:, cols(h)], ALU.subtract)
-                    partner = look_up_partner(t, h)
-                    score = score_tile(t, h)
-                    nc.scalar.activation(score[:], partner[:], ACT.Exp, scale=0.5)
-                    nc.vector.tensor_reduce(tot[:, h * P : (h + 1) * P], score[:].rearrange("p (v d) -> p v d", d=D), mybir.AxisListType.X, ALU.add)
-            nc.vector.scalar_tensor_tensor(
-                ratio[t][:, 0:V], tot[:, 0:V], unit_sb[:, t : t + 1], inverse[t][:], ALU.mult, ALU.mult
-            )
-            for part in range(OUT_PARTS):
-                slots = slice(part * OUT_COLS, (part + 1) * OUT_COLS)
-                window = ratio[t][:].indirect(entries(lib_sb, part * OUT_COLS, OUT_COLS))
-                if (t, part) in ONV:
-                    nc.vector.tensor_copy(picked[:, t, slots], window)
-                else:
-                    nc.scalar.activation(picked[:, t, slots], window, ACT.Copy)
+                nc.scalar.activation(picked[:, t, OUT_COLS:U], second, ACT.Copy)
 
+        w3_grouped = keep.tile([P, N, PACK], BF16, name="w3_grouped", align_bytes=64)
+        nc.gpsimd.tensor_scalar(w3_grouped[:], w3_raw[:].rearrange("p j c -> p c j"), 1.0, 0.0, ALU.mult, ALU.add)
+        w3_codes = keep.tile([P, N], U32, name="w3_codes", tag="inverse", align_bytes=64)
+        w3_scales = keep.tile([P, N], U8, name="w3_scales", align_bytes=64)
+        nc.vector.quantize_mx(out=w3_codes[:].bitcast(FP8X4), scales=w3_scales[:], in_=w3_grouped[:].rearrange("p c j -> p (c j)"))
+
+        hid = keep.tile([P, U, PACK], BF16, name="hid", align_bytes=64)
         for part in range(OUT_PARTS):
             slots = slice(part * OUT_COLS, (part + 1) * OUT_COLS)
-            nc.vector.tensor_copy(out=hid[:, slots, :], in_=picked[:, :, slots].rearrange("p t r -> p r t"))
+            (nc.vector.tensor_copy if part == 0 else nc.scalar.copy)(out=hid[:, slots, :], in_=picked[:, :, slots].rearrange("p t r -> p r t"))
             hid_codes = ring.tile([P, OUT_COLS], U32, name="hid_codes%d" % part, tag="hid_codes", align_bytes=64)
             hid_scales = ring.tile([P, OUT_COLS], U8, name="hid_scales%d" % part, tag="hid_scales", align_bytes=64)
             nc.vector.quantize_mx(out=hid_codes[:].bitcast(FP8X4), scales=hid_scales[:], in_=hid[:, slots, :].rearrange("p r t -> p (r t)"))
-            acc = bank(HALVES * part + 1, "out_acc%d" % part)
+            acc = bank(BANKS - 1 - part, "out_acc%d" % part)
             nc.tensor.matmul_mx(
                 out=acc[:, 0:OUT_COLS],
                 lhsT=w3_codes[:].bitcast(FP8X4),

import math
from contextlib import ExitStack

import concourse.mybir as mybir
from concourse.masks import make_identity

F32 = mybir.dt.float32
BF16 = mybir.dt.bfloat16
I32 = mybir.dt.int32
U32 = mybir.dt.uint32
U16 = mybir.dt.uint16
U8 = mybir.dt.uint8
FP8X4 = mybir.dt.float8_e4m3fn_x4
ACT = mybir.ActivationFunctionType
ALU = mybir.AluOpType

K, T, S, D, N, H, V, U = 1024, 2048, 1024, 4, 128, 512, 256, 512
P = 128
PACK = 4
K_PASS = P * PACK
PASSES = K // K_PASS
QUADRANTS = 4
SCALE_ROWS = 4
TILES = H // P
BANK = 512
HALVES = S // BANK
LIST_ROWS = 16
OUT_PARTS = 2
OUT_COLS = U // OUT_PARTS
LIB_WINDOW = 2 * OUT_COLS
W2_ROWS_ON_VECTOR = 80
LAST_QUANTISE_PIECES = 2
BANKS = 8
PAIRS = 2
SHIFTS_ON_VECTOR = 1
EXPONENT_BANKS = 6
SOFTPLUS_CAP = 40.0
LOG_FLOOR = 2.0**-63

FLOPS = 2 * 2 * K * H * S + 2 * H * N * U


def tile_picked_ybioms_cos_p_kernel(tc, x_words, x_scales, w1, w2, ref, unit, w3, offs, nl, lib, out):
    nc = tc.nc
    with ExitStack() as ctx:
        keep = ctx.enter_context(tc.tile_pool(name="keep", bufs=1))
        ring = ctx.enter_context(tc.tile_pool(name="ring", bufs=2))
        psum = ctx.enter_context(tc.psum_pool(name="psum", bufs=1))

        def bank(index, name):
            return psum.tile([P, BANK], F32, name=name, tag="bank%d" % index)

        def entries(list_tile, first, count):
            return list_tile[:, first // LIST_ROWS : (first + count) // LIST_ROWS]

        def cols(h):
            return slice(h * BANK, (h + 1) * BANK)

        offs_sb = keep.tile([P, S // LIST_ROWS], U16, name="offs_sb")
        nl_sb = keep.tile([P, S // LIST_ROWS], U16, name="nl_sb")
        lib_sb = keep.tile([P, U // LIST_ROWS], U16, name="lib_sb")
        x_table = [keep.tile([P, T], I32, name="x_table%d" % o) for o in range(PASSES)]
        scale_table = keep.tile([P, T], U8, name="scale_table")
        w1_raw = [keep.tile([P, PACK, H], F32, name="w1_raw%d" % o) for o in range(PASSES)]
        w2_raw = [keep.tile([P, PACK, H], F32, name="w2_raw%d" % o) for o in range(PASSES)]
        w3_raw = keep.tile([P, PACK, N], F32, name="w3_raw")
        ref_sb = [keep.tile([P, S], F32, name="ref_sb%d" % t) for t in range(TILES)]
        unit_sb = keep.tile([P, TILES], F32, name="unit_sb")
        identity = keep.tile([P, P], F32, name="identity")
        ratio = [keep.tile([P, LIB_WINDOW], F32, name="ratio%d" % t) for t in range(TILES)]

        def load_x(o):
            nc.sync.dma_start(out=x_table[o][:], in_=x_words[o].rearrange("p n t -> p (n t)").bitcast(I32))

        def load_w(raw, w, o):
            nc.sync.dma_start(out=raw[o][:], in_=w[o * K_PASS : (o + 1) * K_PASS, :].rearrange("(p j) c -> p j c", j=PACK))

        def load_ref(t):
            nc.sync.dma_start(out=ref_sb[t][:], in_=ref.rearrange("(p t) j -> p t j", t=TILES)[:, t, :])

        nc.vector.memset(scale_table[:].bitcast(I32), 0)
        load_x(0)
        nc.sync.dma_start(offs_sb[:], offs)
        for q in range(QUADRANTS):
            nc.sync.dma_start(
                out=scale_table[32 * q : 32 * q + SCALE_ROWS * PASSES, :].bitcast(I32),
                in_=x_scales[:, SCALE_ROWS * q : SCALE_ROWS * (q + 1), :].bitcast(I32),
            )
        load_w(w2_raw, w2, 0)
        load_x(1)
        load_w(w2_raw, w2, 1)
        load_w(w1_raw, w1, 0)
        load_w(w1_raw, w1, 1)
        load_ref(0)
        load_ref(1)
        load_ref(2)
        nc.sync.dma_start(nl_sb[:], nl)
        load_ref(3)
        nc.sync.dma_start(out=w3_raw[:], in_=w3.rearrange("(p j) c -> p j c", j=PACK))
        nc.sync.dma_start(out=unit_sb[:], in_=unit.rearrange("(p t) o -> p (t o)", t=TILES))
        nc.sync.dma_start(lib_sb[:], lib)

        make_identity(nc, identity[:])
        for t in range(TILES):
            nc.gpsimd.memset(ratio[t][:, V:LIB_WINDOW], 0.0)

        x_codes = [keep.tile([P, S], U32, name="x_codes%d" % o, align_bytes=64) for o in range(PASSES)]
        x_planes = keep.tile([P, S], U8, name="x_planes", align_bytes=64)

        def gather_x(o):
            for h in range(HALVES):
                nc.vector.tensor_copy(x_codes[o][:, cols(h)], x_table[o][:].bitcast(U32).indirect(entries(offs_sb, h * BANK, BANK)))

        def round_w(raw, on_vector, name):
            grouped = keep.tile([P, TILES, P, PACK], BF16, name=name, align_bytes=64)
            dst = grouped[:].rearrange("p t m j -> p m j t")
            src = raw[:].rearrange("p j (m t) -> p m j t", t=TILES)
            if on_vector > 0:
                nc.vector.tensor_copy(out=dst[:, 0:on_vector], in_=src[:, 0:on_vector])
            if on_vector < P:
                nc.scalar.copy(out=dst[:, on_vector:P], in_=src[:, on_vector:P])
            return grouped

        def quantize_w(grouped, pieces, name):
            codes = keep.tile([P, H], U32, name=name + "_codes", align_bytes=64)
            scales = keep.tile([P, H], U8, name=name + "_scales", align_bytes=64)
            values = grouped[:].rearrange("p t m j -> p (t m j)")
            width = H // pieces
            for c in range(0, H, width):
                nc.vector.quantize_mx(out=codes[:, c : c + width].bitcast(FP8X4), scales=scales[:, c : c + width], in_=values[:, PACK * c : PACK * (c + width)])
            return codes, scales

        def product(w_mx, t, h, name):
            acc = bank(HALVES * t + h, name)
            for o in range(PASSES):
                codes, scales = w_mx[o]
                nc.tensor.matmul_mx(
                    out=acc[:],
                    lhsT=codes[:, t * P : (t + 1) * P].bitcast(FP8X4),
                    lhsT_scale=scales[:, t * P : (t + 1) * P],
                    rhs=x_codes[o][:, cols(h)].bitcast(FP8X4),
                    rhs_scale=x_planes[SCALE_ROWS * o : P, cols(h)],
                    start=(o == 0),
                    stop=(o == PASSES - 1),
                )
            return acc

        w2_mx = []
        for o in range(PASSES):
            gather_x(o)
            if o == 0:
                nc.vector.tensor_copy(x_planes[:], scale_table[:].indirect(offs_sb[:]))
            w2_mx.append(quantize_w(round_w(w2_raw[o], (0, 32)[o], "w2_grouped%d" % o), 1, "w2_%d" % o))

        mzz = [keep.tile([P, S], F32, name="mzz%d" % t) for t in range(TILES)]
        for t in range(TILES):
            for h in range(HALVES):
                mz = product(w2_mx, t, h, "mz%d_%d" % (t, h))
                nc.scalar.activation(mzz[t][:, cols(h)], mz[:], ACT.Tanh)

        w1_mx = [quantize_w(round_w(w1_raw[0], 64, "w1_grouped0"), 1, "w1_0")]
        w1_mx.append(quantize_w(round_w(w1_raw[1], P, "w1_grouped1"), LAST_QUANTISE_PIECES, "w1_1"))
        shifted_first = keep.tile([P, SHIFTS_ON_VECTOR, S], F32, name="shifted_first", tag="w1_grouped1", align_bytes=64)
        shifted = [shifted_first[:, t] for t in range(SHIFTS_ON_VECTOR)]
        for t in range(SHIFTS_ON_VECTOR):
            nc.vector.tensor_tensor(shifted[t], mzz[t][:], ref_sb[t][:], ALU.subtract)
        shifted_later = keep.tile([P, TILES - SHIFTS_ON_VECTOR, S], F32, name="shifted_later", tag="ref_sb%d" % (SHIFTS_ON_VECTOR - 1))
        shifted.extend([shifted_later[:, t] for t in range(TILES - SHIFTS_ON_VECTOR)])

        soft = [keep.tile([P, S], F32, name="soft%d" % t, align_bytes=64) for t in range(TILES)]
        inten = [keep.tile([P, S], F32, name="inten%d" % t) for t in range(TILES)]
        it = {}
        for t in range(TILES):
            for h in range(HALVES):
                it[t, h] = product(w1_mx, t, h, "it%d_%d" % (t, h))
                nc.scalar.activation(soft[t][:, cols(h)], it[t, h][:], ACT.Exp)

        for t in range(SHIFTS_ON_VECTOR, TILES):
            nc.gpsimd.tensor_tensor(shifted[t], mzz[t][:], ref_sb[t][:], ALU.subtract)
        miss = {}
        for t in range(TILES):
            for h in range(HALVES):
                miss[t, h] = keep.tile([P, BANK], F32, name="miss%d_%d" % (t, h), align_bytes=64)
                nc.vector.tensor_copy(miss[t, h][:], mzz[t][:].indirect(entries(nl_sb, h * BANK, BANK)))
                nc.gpsimd.tensor_tensor(miss[t, h][:], miss[t, h][:], shifted[t][:, cols(h)], ALU.subtract)

        for t in range(TILES):
            nc.scalar.activation(soft[t][:], soft[t][:], ACT.Ln, bias=1.0)
        for t in range(TILES):
            for h in range(HALVES):
                nc.vector.scalar_tensor_tensor(inten[t][:, cols(h)], soft[t][:, cols(h)], SOFTPLUS_CAP, it[t, h][:], ALU.min, ALU.max)

        log_inten = [keep.tile([P, S], F32, name="log_inten%d" % t) for t in range(TILES)]
        exponent = {}

        def turn(dst, src, start, stop):
            nc.tensor.matmul(dst, lhsT=src, rhs=identity[:], is_transpose=True, start=start, stop=stop)

        def add_turned(acc, src, opens):
            for d in range(D):
                turn(acc[:, d * P : (d + 1) * P], src[:, d:BANK:D], opens and d == 0, not opens and d == D - 1)

        def open_exponent(t, h):
            exponent[t, h] = bank(PAIRS + (HALVES * t + h) % EXPONENT_BANKS, "exponent%d_%d" % (t, h))
            add_turned(exponent[t, h], log_inten[t][:, cols(h)], True)

        norm_turned = bank(0, "norm_turned")
        for t in range(PAIRS):
            for h in range(HALVES):
                g = HALVES * t + h
                for d in range(D):
                    turn(norm_turned[:, g * P : (g + 1) * P], inten[t][:, h * BANK + d : (h + 1) * BANK : D], d == 0, d == D - 1)
        inverse = keep.tile([P, TILES, V], F32, name="inverse", align_bytes=64)
        for t in range(PAIRS, TILES):
            nc.vector.tensor_reduce(inverse[:, t], inten[t][:].rearrange("p (v d) -> p v d", d=D), mybir.AxisListType.X, ALU.add)

        def square(t):
            for h in range(HALVES):
                nc.scalar.activation(miss[t, h][:], miss[t, h][:], ACT.Square, scale=math.sqrt(3.0))

        for t in range(TILES):
            nc.scalar.activation(log_inten[t][:], inten[t][:], ACT.Ln, bias=LOG_FLOOR)
            if t > 0:
                square(t - 1)
            if t == PAIRS - 1:
                turned = keep.tile([P, BANK], F32, name="log_norm_turned")
                nc.scalar.activation(turned[:], norm_turned[:], ACT.Ln, bias=0.3)
                log_norm = bank(0, "log_norm")
                for g in range(BANK // P):
                    turn(log_norm[:, g * P : (g + 1) * P], turned[:, g * P : (g + 1) * P], True, True)
            for h in range(HALVES):
                if HALVES * t + h < EXPONENT_BANKS:
                    open_exponent(t, h)
        nc.scalar.activation(inverse[:, PAIRS:TILES], inverse[:, PAIRS:TILES], ACT.Ln, bias=0.3)
        square(TILES - 1)
        nc.scalar.activation(inverse[:, 0:PAIRS].rearrange("p t v -> p (t v)"), log_norm[:], ACT.Exp, scale=-1.0)
        nc.scalar.activation(inverse[:, PAIRS:TILES], inverse[:, PAIRS:TILES], ACT.Exp, scale=-1.0)

        picked = keep.tile([P, TILES, U], BF16, name="picked")
        for t in range(TILES):
            psc = []
            for h in range(HALVES):
                if HALVES * t + h >= EXPONENT_BANKS:
                    open_exponent(t, h)
                partner = ring.tile([P, BANK], F32, name="partner%d_%d" % (t, h), tag="partner", bufs=4)
                nc.vector.tensor_tensor(partner[:], log_inten[t][:].indirect(entries(nl_sb, h * BANK, BANK)), miss[t, h][:], ALU.subtract)
                add_turned(exponent[t, h], partner[:], False)
                psc.append(keep.tile([P, BANK], F32, name="psc%d_%d" % (t, h), tag="psc%d_%d" % (t % 2, h)))
                nc.scalar.activation(psc[h][:], exponent[t, h][:], ACT.Exp, scale=0.5)
            tot = bank((t + 1) % PAIRS, "tot%d" % t)
            for h in range(HALVES):
                for d in range(D):
                    turn(tot[:, h * P : (h + 1) * P], psc[h][:, d * P : (d + 1) * P], d == 0, d == D - 1)
            nc.vector.scalar_tensor_tensor(ratio[t][:, 0:V], tot[:, 0:V], unit_sb[:, t : t + 1], inverse[:, t], ALU.mult, ALU.mult)
            nc.vector.tensor_copy(picked[:, t, 0:OUT_COLS], ratio[t][:].indirect(entries(lib_sb, 0, OUT_COLS)))
            second = ratio[t][:].indirect(entries(lib_sb, OUT_COLS, OUT_COLS))
            if t < 0:
                nc.vector.tensor_copy(picked[:, t, OUT_COLS:U], second)
            else:
                nc.scalar.activation(picked[:, t, OUT_COLS:U], second, ACT.Copy)

        w3_grouped = keep.tile([P, N, PACK], BF16, name="w3_grouped", align_bytes=64)
        nc.gpsimd.tensor_scalar(w3_grouped[:], w3_raw[:].rearrange("p j c -> p c j"), 1.0, 0.0, ALU.mult, ALU.add)
        w3_codes = keep.tile([P, N], U32, name="w3_codes", tag="inverse", align_bytes=64)
        w3_scales = keep.tile([P, N], U8, name="w3_scales", align_bytes=64)
        nc.vector.quantize_mx(out=w3_codes[:].bitcast(FP8X4), scales=w3_scales[:], in_=w3_grouped[:].rearrange("p c j -> p (c j)"))

        hid = keep.tile([P, U, PACK], BF16, name="hid", align_bytes=64)
        for part in range(OUT_PARTS):
            slots = slice(part * OUT_COLS, (part + 1) * OUT_COLS)
            (nc.vector.tensor_copy if part == 0 else nc.scalar.copy)(out=hid[:, slots, :], in_=picked[:, :, slots].rearrange("p t r -> p r t"))
            hid_codes = ring.tile([P, OUT_COLS], U32, name="hid_codes%d" % part, tag="hid_codes", align_bytes=64)
            hid_scales = ring.tile([P, OUT_COLS], U8, name="hid_scales%d" % part, tag="hid_scales", align_bytes=64)
            nc.vector.quantize_mx(out=hid_codes[:].bitcast(FP8X4), scales=hid_scales[:], in_=hid[:, slots, :].rearrange("p r t -> p (r t)"))
            acc = bank(BANKS - 1 - part, "out_acc%d" % part)
            nc.tensor.matmul_mx(
                out=acc[:, 0:OUT_COLS],
                lhsT=w3_codes[:].bitcast(FP8X4),
                lhsT_scale=w3_scales[:],
                rhs=hid_codes[:].bitcast(FP8X4),
                rhs_scale=hid_scales[:],
                start=True,
                stop=True,
            )
            result = ring.tile([P, OUT_COLS], F32, name="result%d" % part, tag="result")
            nc.scalar.copy(out=result[:], in_=acc[:, 0:OUT_COLS])
            nc.sync.dma_start(out=out[:, slots], in_=result[:])
